import numpy as np
import ml_dtypes


def mxq(x, axis, fmt="e4m3"):
    dtype, down = {"e4m3": (ml_dtypes.float8_e4m3fn, 7), "e5m2": (ml_dtypes.float8_e5m2, 14)}[fmt]
    v = np.moveaxis(np.asarray(x, np.float32).astype(ml_dtypes.bfloat16).astype(np.float64), axis, -1)
    blocks = v.reshape(v.shape[:-1] + (-1, 32))
    amax = np.abs(blocks).max(-1, keepdims=True)
    byte = np.maximum(np.where(amax > 0, np.frexp(amax)[1] - 1 + 127, 0) - down, 1)
    scale = np.exp2(byte - 127.0)
    codes = (blocks / scale).astype(np.float32).astype(dtype).astype(np.float64)
    return np.moveaxis((codes * scale).reshape(v.shape), -1, axis)


WIDE = False


def mx_kscale(k, group=512):
    if not WIDE:
        return np.ones(k)
    levels = np.array([18, -18])
    if group != 512:
        return np.exp2(np.random.permutation(np.resize(levels, k // group))).repeat(group)
    if k % 512:
        return np.exp2(np.random.permutation(np.resize(levels, k // 32))).repeat(32)
    a = np.empty((k // 512, 16))
    for p in range(k // 512):
        a[p, :8] = np.random.permutation(np.resize(levels, 8))
        for g in range(8):
            far = levels[np.abs(levels - a[p, g]) >= 10]
            a[p, g + 8] = far[np.random.randint(len(far))]
    return np.exp2(a.ravel()).repeat(32)


def f64(x):
    return np.asarray(x).astype(np.float64)


def softplus(v):
    return np.log(1.0 + np.exp(v))


def sigmoid(v):
    return 1.0 / (1.0 + np.exp(-v))


G, D, M, N = 4, 128, 128, 512


def setup_inputs():
    n = np.random.standard_normal
    s_d = mx_kscale(D, 0)
    return {
        "x": (n((G, D, N)) * s_d[:, None]).astype(np.float32),
        "w1": (n((G, D, M)) / np.sqrt(D) / s_d[:, None]).astype(np.float32),
        "w2": (n((G, D, M)) / np.sqrt(D) / s_d[:, None]).astype(np.float32),
        "gn": (np.random.uniform(0.5, 2.0, (G, M, 1))).astype(np.float32),
        "dx": (n((G, D, N)) * s_d[:, None]).astype(np.float32),
        "og": (np.random.uniform(0.5, 2.0, (G, M, 1))).astype(np.float32),
        "base": (0.3 * n((G, M, N))).astype(np.float32),
    }


def reference(x, w1, w2, gn, dx, og, base):
    w1q = mxq(f64(w1), 1, "e4m3")
    xq = mxq(f64(x), 1, "e4m3")
    z1 = w1q.transpose(0, 2, 1) @ xq
    dxq = mxq(f64(dx), 1, "e4m3")
    tz1 = w1q.transpose(0, 2, 1) @ dxq
    w2q = mxq(f64(w2), 1, "e4m3")
    z2 = w2q.transpose(0, 2, 1) @ xq
    tz2 = w2q.transpose(0, 2, 1) @ dxq
    sp = softplus(z1) * softplus(z2)
    xsp = tz1 * sigmoid(z1) * softplus(z2) + tz2 * sigmoid(z2) * softplus(z1)
    xh = xsp * f64(gn) / (sp * f64(gn) + 1.0) * sigmoid(z1 - z2) + (tz1 - tz2) * sigmoid(z1 - z2) * (1.0 - sigmoid(z1 - z2)) * np.log(sp * f64(gn) + 1.0)
    y = xh * f64(og) + f64(base)
    return y

@@ -1,0 +1,225 @@
+from contextlib import ExitStack
+import concourse.mybir as mybir
+
+F32 = mybir.dt.float32
+BF16 = mybir.dt.bfloat16
+U32 = mybir.dt.uint32
+U8 = mybir.dt.uint8
+FP8X4 = mybir.dt.float8_e4m3fn_x4
+ALU = mybir.AluOpType
+ACT = mybir.ActivationFunctionType
+
+G, D, M, N = 4, 128, 128, 512
+P = 128
+R = 32
+PACK = 4
+W = 256
+NMM = 128
+TINY = 2.0 ** -40
+FLOPS = 4 * 2 * G * D * M * N
+POOL = True
+
+
+def tile_rows_tnsoftprod_kernel(tc, x, w1, w2, gn, dx, og, base, out):
+    nc = tc.nc
+    with ExitStack() as ctx:
+        sb = ctx.enter_context(tc.tile_pool(name="sb", bufs=1))
+        ps = ctx.enter_context(tc.psum_pool(name="ps", bufs=1))
+        ctx.enter_context(tc.manual_schedule())
+
+        def f32(name, *shape):
+            return sb.tile([P, *shape], F32, name=name, align_bytes=64)
+
+        def operand(name, width):
+            return dict(
+                raw=f32(name + "_raw", PACK, width),
+                grouped=sb.tile([P, width, PACK], BF16, name=name + "_bf", align_bytes=64),
+                codes=sb.tile([P, width], U32, name=name + "_codes", align_bytes=64),
+                scales=sb.tile([P, width], U8, name=name + "_scales", align_bytes=64),
+            )
+
+        def load(op, src, cols):
+            nc.sync.dma_start(out=op["raw"][:], in_=src.rearrange("g (p j) n -> (g p) j n", j=PACK)[:, :, cols])
+
+        def cast(op, pool=False):
+            dst = op["grouped"][:].rearrange("p (c i) j -> p c j i", i=4)
+            src = op["raw"][:].rearrange("p j (c i) -> p c j i", i=4)
+            if pool:
+                nc.gpsimd.tensor_scalar(out=op["grouped"][:], in0=op["raw"][:].rearrange("p j n -> p n j"), scalar1=1.0, scalar2=0.0, op0=ALU.mult, op1=ALU.add)
+            else:
+                nc.vector.tensor_copy(out=dst, in_=src)
+
+        def quant(op):
+            nc.vector.quantize_mx(out=op["codes"][:].bitcast(FP8X4), scales=op["scales"][:], in_=op["grouped"][:].rearrange("p n j -> p (n j)"))
+
+        def products(banks, gs, mov):
+            for k, wt in enumerate(ws):
+                for c in range(0, W, NMM):
+                    for g in gs:
+                        rows = slice(R * g, R * g + R)
+                        nc.tensor.matmul_mx(out=banks[g][:, k * W + c : k * W + c + NMM],
+                            lhsT=wt["codes"][rows, :].bitcast(FP8X4), lhsT_scale=wt["scales"][rows, :],
+                            rhs=mov["codes"][rows, c : c + NMM].bitcast(FP8X4), rhs_scale=mov["scales"][rows, c : c + NMM],
+                            start=True, stop=True)
+
+        ws = [operand("w1", M), operand("w2", M)]
+        xs = [operand("x%d" % h, W) for h in range(2)]
+        dxs = [operand("dx%d" % h, W) for h in range(2)]
+        zb = [ps.tile([P, 2 * W], F32, name="z%d" % g) for g in range(G)]
+        tb = [ps.tile([P, 2 * W], F32, name="t%d" % g) for g in range(G)]
+        gn_sb = f32("gn_sb", G, 8)
+        og_sb = f32("og_sb", G, 8)
+        cc = f32("cc", G, 8)
+        oq = f32("oq", G, 8)
+        names1 = ["cb", "ct", "d", "s", "dt", "m", "L", "r", "u", "v", "bs"]
+        T = [{k: f32("%s%d" % (k, h), G, W) for k in names1} for h in range(2)]
+        for h in range(2):
+            for k in ["q", "p", "xy"]:
+                T[h][k] = f32("%s%d" % (k, h), G, 2, W)
+        cols = [slice(h * W, h * W + W) for h in range(2)]
+
+        load(xs[0], x, cols[0])
+        load(ws[0], w1, slice(0, M))
+        load(ws[1], w2, slice(0, M))
+        load(dxs[0], dx, cols[0])
+        load(xs[1], x, cols[1])
+        load(dxs[1], dx, cols[1])
+        with nc.allow_non_contiguous_dma(reason="one gain to a partition"):
+            nc.sync.dma_start(out=og_sb[:, :, 0:1], in_=og.rearrange("g m o -> m g o"))
+            nc.sync.dma_start(out=gn_sb[:, :, 0:1], in_=gn.rearrange("g m o -> m g o"))
+        for h in range(2):
+            nc.sync.dma_start(out=T[h]["bs"][:], in_=base.rearrange("g m n -> m g n")[:, :, cols[h]])
+
+        cast(xs[0]); cast(ws[0]); quant(xs[0]); cast(ws[1]); quant(ws[0]); quant(ws[1])
+        products(zb, (0, 1), xs[0]); products(zb, (2, 3), xs[0])
+
+        def qact(h, g):
+            nc.scalar.activation(out=T[h]["q"][:, g].rearrange("p k n -> p (k n)"), in_=zb[g][:], func=ACT.Sigmoid, scale=-1.0)
+
+        def cb(h, g):
+            nc.scalar.copy(out=T[h]["cb"][:, g], in_=zb[g][:, W:])
+
+        def ct(h, g):
+            nc.scalar.activation(out=T[h]["ct"][:, g], in_=tb[g][:, W:], func=ACT.Copy, scale=oq[:, g, 0:1])
+
+        def dd(h, g):
+            t = T[h]
+            nc.vector.tensor_tensor(out=t["d"][:, g], in0=zb[g][:, :W], in1=t["cb"][:, g], op=ALU.subtract)
+
+        def dt(h, g):
+            t = T[h]
+            nc.vector.scalar_tensor_tensor(out=t["dt"][:, g], in0=tb[g][:, :W], scalar=oq[:, g, 0:1], in1=t["ct"][:, g], op0=ALU.mult, op1=ALU.subtract)
+
+        def xy(h, g):
+            t = T[h]
+            nc.vector.scalar_tensor_tensor(out=t["xy"][:, g].rearrange("p k n -> p (k n)"), in0=t["q"][:, g].rearrange("p k n -> p (k n)"), scalar=1.0, in1=tb[g][:], op0=ALU.subtract, op1=ALU.mult)
+
+        def gate(h, gs):
+            nc.scalar.activation(out=T[h]["s"][:, gs], in_=T[h]["d"][:, gs], func=ACT.Tanh, scale=0.5)
+
+        def logq(h, g):
+            nc.scalar.activation(out=T[h]["p"][:, g], in_=T[h]["q"][:, g], func=ACT.Ln, bias=TINY)
+
+        def soft(h, g):
+            v = T[h]["p"][:, g].rearrange("p k n -> p (k n)")
+            nc.vector.scalar_tensor_tensor(out=v, in0=zb[g][:], scalar=-1.0, in1=v, op0=ALU.mult, op1=ALU.min)
+
+        def tt(eng, o, a, b, op):
+            eng.tensor_tensor(out=o, in0=a, in1=b, op=op)
+
+        def prod(h, gs, eng):
+            t = T[h]
+            tt(eng, t["m"][:, gs], t["p"][:, gs, 0], t["p"][:, gs, 1], ALU.mult)
+
+        def logs(h, g):
+            t = T[h]
+            nc.scalar.activation(out=t["L"][:, g], in_=t["m"][:, g], func=ACT.Ln, scale=gn_sb[:, g, 0:1], bias=1.0)
+
+        def recip(h, gs):
+            t = T[h]
+            nc.scalar.activation(out=t["r"][:, gs], in_=t["L"][:, gs], func=ACT.Exp, scale=-1.0)
+
+        def cu(h, gs, eng):
+            t = T[h]
+            tt(eng, t["u"][:, gs], t["xy"][:, gs, 0], t["p"][:, gs, 1], ALU.mult)
+
+        def cv(h, gs, eng):
+            t = T[h]
+            tt(eng, t["v"][:, gs], t["xy"][:, gs, 1], t["p"][:, gs, 0], ALU.mult)
+
+        def csum(h, gs, eng):
+            t = T[h]
+            tt(eng, t["u"][:, gs], t["u"][:, gs], t["v"][:, gs], ALU.add)
+
+        def bterm(h, gs):
+            t = T[h]
+            nc.vector.scalar_tensor_tensor(out=t["m"][:, gs], in0=t["s"][:, gs], scalar=1.0, in1=t["L"][:, gs], op0=ALU.subtract, op1=ALU.mult)
+
+        def bterm2(h, gs, eng):
+            t = T[h]
+            tt(eng, t["dt"][:, gs], t["dt"][:, gs], t["m"][:, gs], ALU.mult)
+
+        def wr(h, g):
+            t = T[h]
+            nc.vector.scalar_tensor_tensor(out=t["u"][:, g], in0=t["u"][:, g], scalar=cc[:, g, 0:1], in1=t["r"][:, g], op0=ALU.mult, op1=ALU.mult)
+
+        def fin(k, h, gs, eng):
+            t = T[h]
+            other, op = [("dt", ALU.subtract), ("s", ALU.mult), ("bs", ALU.add)][k]
+            if k == 1:
+                eng.scalar_tensor_tensor(out=t["u"][:, gs], in0=t["s"][:, gs], scalar=1.0, in1=t["u"][:, gs], op0=ALU.add, op1=ALU.mult)
+            else:
+                tt(eng, t["u"][:, gs], t["u"][:, gs], t[other][:, gs], op)
+
+        def store(h, gs):
+            nc.sync.dma_start(out=out.rearrange("g m n -> m g n")[:, gs, cols[h]], in_=T[h]["u"][:, gs])
+
+
+        A, B, ALL = slice(0, 2), slice(2, 4), slice(0, 4)
+        V = nc.vector
+        PL = nc.gpsimd if POOL else V
+        cast(dxs[0]); quant(dxs[0])
+        products(tb, (0, 1), dxs[0]); products(tb, (2, 3), dxs[0])
+        for g in range(G):
+            qact(0, g)
+        cast(xs[1]); xy(0, 0); quant(xs[1]); xy(0, 1); cast(dxs[1]); xy(0, 2)
+        V.tensor_scalar(out=oq[:, :, 0:1], in0=og_sb[:, :, 0:1], scalar1=0.25, scalar2=None, op0=ALU.mult)
+        V.scalar_tensor_tensor(out=cc[:, :, 0:1], in0=gn_sb[:, :, 0:1], scalar=0.5, in1=og_sb[:, :, 0:1], op0=ALU.mult, op1=ALU.mult)
+
+        def log_phase(h):
+            for g in range(G):
+                logq(h, g)
+            soft(h, 0); soft(h, 1); prod(h, A, PL); soft(h, 2); soft(h, 3); prod(h, B, PL); cu(h, A, PL)
+            xy(h, 3)
+            for g in range(G):
+                cb(h, g); dd(h, g)
+                if g % 2 and h == 0:
+                    products(zb, (g - 1, g), xs[1])
+            for g in range(G):
+                ct(h, g); dt(h, g)
+            for g in range(G):
+                logs(h, g)
+
+        def mid(h):
+            cv(h, A, V); cu(h, B, V); cv(h, B, V); csum(h, A, V); csum(h, B, V)
+            gate(h, A); recip(h, A); gate(h, B); recip(h, B)
+
+        log_phase(0)
+        quant(dxs[1])
+        products(tb, (0, 1, 2, 3), dxs[1])
+        mid(0)
+        bterm(0, A); wr(0, 0); wr(0, 1); bterm2(0, A, V); bterm(0, B); fin(0, 0, A, V); wr(0, 2); wr(0, 3); bterm2(0, B, V); fin(1, 0, A, V)
+        for g in range(G):
+            qact(1, g)
+        fin(2, 0, A, PL)
+        xy(1, 0); xy(1, 1); xy(1, 2)
+        fin(0, 0, B, V); fin(1, 0, B, V)
+        fin(2, 0, B, PL)
+        store(0, ALL)
+        log_phase(1)
+        mid(1)
+        bterm(1, A); wr(1, 0); wr(1, 1); bterm2(1, A, V); bterm(1, B); fin(0, 1, A, V); wr(1, 2); wr(1, 3); fin(1, 1, A, V); bterm2(1, B, V); fin(2, 1, A, V)
+        store(1, A)
+        for k in range(3):
+            fin(k, 1, slice(2, 3), V); fin(k, 1, slice(3, 4), V)
+        store(1, slice(2, 3)); store(1, slice(3, 4))

@@ -67,28 +67,30 @@ def tile_rows_tnsoftprod_kernel(tc, x, w1, w2, gn, dx, og, base, out):
         dxs = [operand("dx%d" % h, W) for h in range(2)]
         zb = [ps.tile([P, 2 * W], F32, name="z%d" % g) for g in range(G)]
         tb = [ps.tile([P, 2 * W], F32, name="t%d" % g) for g in range(G)]
-        gn_sb = f32("gn_sb", G, 8)
-        og_sb = f32("og_sb", G, 8)
+        gains_rows = f32("gains_rows", 2 * M)
+        gains = f32("gains", 2 * M)
+        gn_sb = gains[:, :M].rearrange("p (g i) -> p g i", g=G)
+        og_sb = gains[:, M:].rearrange("p (g i) -> p g i", g=G)
+        bs = f32("bs", G, N)
         cc = f32("cc", G, 8)
         oq = f32("oq", G, 8)
-        names1 = ["cb", "ct", "d", "s", "dt", "m", "L", "r", "u", "v", "bs"]
+        names1 = ["cb", "ct", "d", "s", "dt", "m", "L", "r", "u", "v"]
         T = [{k: f32("%s%d" % (k, h), G, W) for k in names1} for h in range(2)]
         for h in range(2):
             for k in ["q", "p", "xy"]:
                 T[h][k] = f32("%s%d" % (k, h), G, 2, W)
         cols = [slice(h * W, h * W + W) for h in range(2)]
 
+        nc.vector.memset(gains_rows[:], 0.0)
+        for k, src in enumerate((gn, og)):
+            nc.scalar.dma_start(out=gains_rows[0:P:R, k * M : k * M + M].rearrange("q (g i) -> q g i", g=G), in_=src.rearrange("g (q i) o -> q g (i o)", i=R))
         load(xs[0], x, cols[0])
         load(ws[0], w1, slice(0, M))
         load(ws[1], w2, slice(0, M))
         load(dxs[0], dx, cols[0])
         load(xs[1], x, cols[1])
         load(dxs[1], dx, cols[1])
-        with nc.allow_non_contiguous_dma(reason="one gain to a partition"):
-            nc.sync.dma_start(out=og_sb[:, :, 0:1], in_=og.rearrange("g m o -> m g o"))
-            nc.sync.dma_start(out=gn_sb[:, :, 0:1], in_=gn.rearrange("g m o -> m g o"))
-        for h in range(2):
-            nc.sync.dma_start(out=T[h]["bs"][:], in_=base.rearrange("g m n -> m g n")[:, :, cols[h]])
+        nc.sync.dma_start(out=bs[:], in_=base.rearrange("g m n -> m g n"))
 
         cast(xs[0]); cast(ws[0]); quant(xs[0]); cast(ws[1]); quant(ws[0]); quant(ws[1])
         products(zb, (0, 1), xs[0]); products(zb, (2, 3), xs[0])
@@ -100,7 +102,7 @@ def tile_rows_tnsoftprod_kernel(tc, x, w1, w2, gn, dx, og, base, out):
             nc.scalar.copy(out=T[h]["cb"][:, g], in_=zb[g][:, W:])
 
         def ct(h, g):
-            nc.scalar.activation(out=T[h]["ct"][:, g], in_=tb[g][:, W:], func=ACT.Copy, scale=oq[:, g, 0:1])
+            nc.scalar.copy(out=T[h]["ct"][:, g], in_=tb[g][:, W:])
 
         def dd(h, g):
             t = T[h]
@@ -108,7 +110,7 @@ def tile_rows_tnsoftprod_kernel(tc, x, w1, w2, gn, dx, og, base, out):
 
         def dt(h, g):
             t = T[h]
-            nc.vector.scalar_tensor_tensor(out=t["dt"][:, g], in0=tb[g][:, :W], scalar=oq[:, g, 0:1], in1=t["ct"][:, g], op0=ALU.mult, op1=ALU.subtract)
+            nc.vector.tensor_tensor(out=t["dt"][:, g], in0=tb[g][:, :W], in1=t["ct"][:, g], op=ALU.subtract)
 
         def xy(h, g):
             t = T[h]
@@ -155,9 +157,9 @@ def tile_rows_tnsoftprod_kernel(tc, x, w1, w2, gn, dx, og, base, out):
             t = T[h]
             nc.vector.scalar_tensor_tensor(out=t["m"][:, gs], in0=t["s"][:, gs], scalar=1.0, in1=t["L"][:, gs], op0=ALU.subtract, op1=ALU.mult)
 
-        def bterm2(h, gs, eng):
+        def bterm2(h, g):
             t = T[h]
-            tt(eng, t["dt"][:, gs], t["dt"][:, gs], t["m"][:, gs], ALU.mult)
+            nc.vector.scalar_tensor_tensor(out=t["dt"][:, g], in0=t["dt"][:, g], scalar=oq[:, g, 0:1], in1=t["m"][:, g], op0=ALU.mult, op1=ALU.mult)
 
         def wr(h, g):
             t = T[h]
@@ -165,11 +167,11 @@ def tile_rows_tnsoftprod_kernel(tc, x, w1, w2, gn, dx, og, base, out):
 
         def fin(k, h, gs, eng):
             t = T[h]
-            other, op = [("dt", ALU.subtract), ("s", ALU.mult), ("bs", ALU.add)][k]
+            other, op = [(t["dt"][:, gs], ALU.subtract), (None, None), (bs[:, gs, cols[h]], ALU.add)][k]
             if k == 1:
                 eng.scalar_tensor_tensor(out=t["u"][:, gs], in0=t["s"][:, gs], scalar=1.0, in1=t["u"][:, gs], op0=ALU.add, op1=ALU.mult)
             else:
-                tt(eng, t["u"][:, gs], t["u"][:, gs], t[other][:, gs], op)
+                tt(eng, t["u"][:, gs], t["u"][:, gs], other, op)
 
         def store(h, gs):
             nc.sync.dma_start(out=out.rearrange("g m n -> m g n")[:, gs, cols[h]], in_=T[h]["u"][:, gs])
@@ -178,13 +180,15 @@ def tile_rows_tnsoftprod_kernel(tc, x, w1, w2, gn, dx, og, base, out):
         A, B, ALL = slice(0, 2), slice(2, 4), slice(0, 4)
         V = nc.vector
         PL = nc.gpsimd if POOL else V
-        cast(dxs[0]); quant(dxs[0])
+        V.transpose(out=gains[:], in_=gains_rows[:])
+        cast(dxs[0])
+        V.tensor_scalar(out=oq[:, :, 0:1], in0=og_sb[:, :, 0:1], scalar1=0.25, scalar2=None, op0=ALU.mult)
+        V.scalar_tensor_tensor(out=cc[:, :, 0:1], in0=gn_sb[:, :, 0:1], scalar=0.5, in1=og_sb[:, :, 0:1], op0=ALU.mult, op1=ALU.mult)
+        quant(dxs[0])
         products(tb, (0, 1), dxs[0]); products(tb, (2, 3), dxs[0])
         for g in range(G):
             qact(0, g)
         cast(xs[1]); xy(0, 0); quant(xs[1]); xy(0, 1); cast(dxs[1]); xy(0, 2)
-        V.tensor_scalar(out=oq[:, :, 0:1], in0=og_sb[:, :, 0:1], scalar1=0.25, scalar2=None, op0=ALU.mult)
-        V.scalar_tensor_tensor(out=cc[:, :, 0:1], in0=gn_sb[:, :, 0:1], scalar=0.5, in1=og_sb[:, :, 0:1], op0=ALU.mult, op1=ALU.mult)
 
         def log_phase(h):
             for g in range(G):
@@ -201,14 +205,14 @@ def tile_rows_tnsoftprod_kernel(tc, x, w1, w2, gn, dx, og, base, out):
                 logs(h, g)
 
         def mid(h):
-            cv(h, A, V); cu(h, B, V); cv(h, B, V); csum(h, A, V); csum(h, B, V)
+            cv(h, ALL, V); cu(h, B, V); csum(h, A, V); csum(h, B, V)
             gate(h, A); recip(h, A); gate(h, B); recip(h, B)
 
         log_phase(0)
         quant(dxs[1])
         products(tb, (0, 1, 2, 3), dxs[1])
         mid(0)
-        bterm(0, A); wr(0, 0); wr(0, 1); bterm2(0, A, V); bterm(0, B); fin(0, 0, A, V); wr(0, 2); wr(0, 3); bterm2(0, B, V); fin(1, 0, A, V)
+        bterm(0, A); wr(0, 0); wr(0, 1); bterm2(0, 0); bterm2(0, 1); bterm(0, B); fin(0, 0, A, V); wr(0, 2); wr(0, 3); bterm2(0, 2); bterm2(0, 3); fin(1, 0, A, V)
         for g in range(G):
             qact(1, g)
         fin(2, 0, A, PL)
@@ -218,7 +222,7 @@ def tile_rows_tnsoftprod_kernel(tc, x, w1, w2, gn, dx, og, base, out):
         store(0, ALL)
         log_phase(1)
         mid(1)
-        bterm(1, A); wr(1, 0); wr(1, 1); bterm2(1, A, V); bterm(1, B); fin(0, 1, A, V); wr(1, 2); wr(1, 3); fin(1, 1, A, V); bterm2(1, B, V); fin(2, 1, A, V)
+        bterm(1, A); wr(1, 0); wr(1, 1); bterm2(1, 0); bterm2(1, 1); bterm(1, B); fin(0, 1, A, V); wr(1, 2); wr(1, 3); fin(1, 1, A, V); bterm2(1, 2); bterm2(1, 3); fin(2, 1, A, V)
         store(1, A)
         for k in range(3):
             fin(k, 1, slice(2, 3), V); fin(k, 1, slice(3, 4), V)

@@ -1,4 +1,5 @@
 from contextlib import ExitStack
+
 import concourse.mybir as mybir
 
 F32 = mybir.dt.float32
@@ -10,18 +11,20 @@ ALU = mybir.AluOpType
 ACT = mybir.ActivationFunctionType
 
 G, D, M, N = 4, 128, 128, 512
+FLOPS = 4 * 2 * G * D * M * N
+
 P = 128
-R = 32
+ROWS = 32
 PACK = 4
 W = 256
-NMM = 128
-TINY = 2.0 ** -40
-FLOPS = 4 * 2 * G * D * M * N
-POOL = True
+N_MM = 128
+TINY = 2.0**-40
+VECTOR_COPIES = 2
 
 
 def tile_rows_tnsoftprod_kernel(tc, x, w1, w2, gn, dx, og, base, out):
     nc = tc.nc
+    vec, act, gps = nc.vector, nc.scalar, nc.gpsimd
     with ExitStack() as ctx:
         sb = ctx.enter_context(tc.tile_pool(name="sb", bufs=1))
         ps = ctx.enter_context(tc.psum_pool(name="ps", bufs=1))
@@ -38,192 +41,292 @@ def tile_rows_tnsoftprod_kernel(tc, x, w1, w2, gn, dx, og, base, out):
                 scales=sb.tile([P, width], U8, name=name + "_scales", align_bytes=64),
             )
 
-        def load(op, src, cols):
-            nc.sync.dma_start(out=op["raw"][:], in_=src.rearrange("g (p j) n -> (g p) j n", j=PACK)[:, :, cols])
+        def load(opnd, src, cols):
+            rows = src.rearrange("g (p j) n -> (g p) j n", j=PACK)
+            nc.sync.dma_start(out=opnd["raw"][:], in_=rows[:, :, cols])
 
-        def cast(op, pool=False):
-            dst = op["grouped"][:].rearrange("p (c i) j -> p c j i", i=4)
-            src = op["raw"][:].rearrange("p j (c i) -> p c j i", i=4)
-            if pool:
-                nc.gpsimd.tensor_scalar(out=op["grouped"][:], in0=op["raw"][:].rearrange("p j n -> p n j"), scalar1=1.0, scalar2=0.0, op0=ALU.mult, op1=ALU.add)
-            else:
-                nc.vector.tensor_copy(out=dst, in_=src)
+        def interleave(opnd):
+            vec.tensor_copy(
+                out=opnd["grouped"][:].rearrange("p (c i) j -> p c j i", i=4),
+                in_=opnd["raw"][:].rearrange("p j (c i) -> p c j i", i=4),
+            )
 
-        def quant(op):
-            nc.vector.quantize_mx(out=op["codes"][:].bitcast(FP8X4), scales=op["scales"][:], in_=op["grouped"][:].rearrange("p n j -> p (n j)"))
+        def interleave_on_gpsimd(opnd):
+            gps.tensor_scalar(
+                out=opnd["grouped"][:],
+                in0=opnd["raw"][:].rearrange("p j n -> p n j"),
+                scalar1=1.0,
+                scalar2=0.0,
+                op0=ALU.mult,
+                op1=ALU.add,
+            )
 
-        def products(banks, gs, mov):
-            for k, wt in enumerate(ws):
-                for c in range(0, W, NMM):
-                    for g in gs:
-                        rows = slice(R * g, R * g + R)
-                        nc.tensor.matmul_mx(out=banks[g][:, k * W + c : k * W + c + NMM],
-                            lhsT=wt["codes"][rows, :].bitcast(FP8X4), lhsT_scale=wt["scales"][rows, :],
-                            rhs=mov["codes"][rows, c : c + NMM].bitcast(FP8X4), rhs_scale=mov["scales"][rows, c : c + NMM],
-                            start=True, stop=True)
+        def quantise(opnd):
+            vec.quantize_mx(
+                out=opnd["codes"][:].bitcast(FP8X4),
+                scales=opnd["scales"][:],
+                in_=opnd["grouped"][:].rearrange("p n j -> p (n j)"),
+            )
 
-        ws = [operand("w1", M), operand("w2", M)]
-        xs = [operand("x%d" % h, W) for h in range(2)]
-        dxs = [operand("dx%d" % h, W) for h in range(2)]
-        zb = [ps.tile([P, 2 * W], F32, name="z%d" % g) for g in range(G)]
-        tb = [ps.tile([P, 2 * W], F32, name="t%d" % g) for g in range(G)]
-        gains_rows = f32("gains_rows", 2 * M)
-        gains = f32("gains", 2 * M)
-        gn_sb = gains[:, :M].rearrange("p (g i) -> p g i", g=G)
-        og_sb = gains[:, M:].rearrange("p (g i) -> p g i", g=G)
-        bs = f32("bs", G, N)
-        cc = f32("cc", G, 8)
-        oq = f32("oq", G, 8)
-        names1 = ["cb", "ct", "d", "s", "dt", "m", "L", "r", "u", "v"]
-        T = [{k: f32("%s%d" % (k, h), G, W) for k in names1} for h in range(2)]
-        for h in range(2):
-            for k in ["q", "p", "xy"]:
-                T[h][k] = f32("%s%d" % (k, h), G, 2, W)
+        def products(banks, groups, moving, first=0, width=W):
+            for k, weight in enumerate(weights):
+                for c in range(0, width, N_MM):
+                    for g in groups:
+                        rows = slice(ROWS * g, ROWS * g + ROWS)
+                        at = k * W + first + c
+                        nc.tensor.matmul_mx(
+                            out=banks[g][:, at : at + N_MM],
+                            lhsT=weight["codes"][rows, :].bitcast(FP8X4),
+                            lhsT_scale=weight["scales"][rows, :],
+                            rhs=moving["codes"][rows, c : c + N_MM].bitcast(FP8X4),
+                            rhs_scale=moving["scales"][rows, c : c + N_MM],
+                            start=True,
+                            stop=True,
+                        )
+
+        weights = [operand("w1", M), operand("w2", M)]
+        x_first = [operand("xa", N_MM), operand("xb", N_MM)]
+        x_second = operand("x1", W)
+        dxs = [operand("dx0", W), operand("dx1", W)]
+        z_bank = [ps.tile([P, 2 * W], F32, name="z%d" % g) for g in range(G)]
+        tz_bank = [ps.tile([P, 2 * W], F32, name="t%d" % g) for g in range(G)]
         cols = [slice(h * W, h * W + W) for h in range(2)]
 
-        nc.vector.memset(gains_rows[:], 0.0)
-        for k, src in enumerate((gn, og)):
-            nc.scalar.dma_start(out=gains_rows[0:P:R, k * M : k * M + M].rearrange("q (g i) -> q g i", g=G), in_=src.rearrange("g (q i) o -> q g (i o)", i=R))
-        load(xs[0], x, cols[0])
-        load(ws[0], w1, slice(0, M))
-        load(ws[1], w2, slice(0, M))
-        load(dxs[0], dx, cols[0])
-        load(xs[1], x, cols[1])
-        load(dxs[1], dx, cols[1])
-        nc.sync.dma_start(out=bs[:], in_=base.rearrange("g m n -> m g n"))
+        gains_rows = f32("gains_rows", 2 * M)
+        gains = f32("gains", 2 * M)
+        gn_col = gains[:, :M].rearrange("p (g i) -> p g i", g=G)
+        og_col = gains[:, M:].rearrange("p (g i) -> p g i", g=G)
+        half_gn_og = f32("cc", G, 8)
+        quarter_og = f32("oq", G, 8)
+        base_sb = f32("bs", G, N)
 
-        cast(xs[0]); cast(ws[0]); quant(xs[0]); cast(ws[1]); quant(ws[0]); quant(ws[1])
-        products(zb, (0, 1), xs[0]); products(zb, (2, 3), xs[0])
+        work = []
+        for h in range(2):
+            tiles = {k: f32("%s%d" % (k, h), G, W) for k in ("z2", "tz2", "dz", "th", "dtz", "sp", "lg", "inv", "acc", "cross")}
+            for k in ("q", "nsp", "nts"):
+                tiles[k] = f32("%s%d" % (k, h), G, 2, W)
+            work.append(tiles)
 
-        def qact(h, g):
-            nc.scalar.activation(out=T[h]["q"][:, g].rearrange("p k n -> p (k n)"), in_=zb[g][:], func=ACT.Sigmoid, scale=-1.0)
+        def pair(tile, g):
+            return tile[:, g].rearrange("p k n -> p (k n)")
 
-        def cb(h, g):
-            nc.scalar.copy(out=T[h]["cb"][:, g], in_=zb[g][:, W:])
+        def sigmoid_piece(g, first):
+            z = z_bank[g][:].rearrange("p (k n) -> p k n", k=2)
+            piece = slice(first, first + N_MM)
+            act.activation(out=work[0]["q"][:, g, :, piece], in_=z[:, :, piece], func=ACT.Sigmoid, scale=-1.0)
 
-        def ct(h, g):
-            nc.scalar.copy(out=T[h]["ct"][:, g], in_=tb[g][:, W:])
+        def sigmoid(h, g):
+            act.activation(out=pair(work[h]["q"], g), in_=z_bank[g][:], func=ACT.Sigmoid, scale=-1.0)
 
-        def dd(h, g):
-            t = T[h]
-            nc.vector.tensor_tensor(out=t["d"][:, g], in0=zb[g][:, :W], in1=t["cb"][:, g], op=ALU.subtract)
+        def log_q(h, g):
+            act.activation(out=work[h]["nsp"][:, g], in_=work[h]["q"][:, g], func=ACT.Ln, bias=TINY)
 
-        def dt(h, g):
-            t = T[h]
-            nc.vector.tensor_tensor(out=t["dt"][:, g], in0=tb[g][:, :W], in1=t["ct"][:, g], op=ALU.subtract)
+        def softplus(h, g):
+            nsp = pair(work[h]["nsp"], g)
+            vec.scalar_tensor_tensor(out=nsp, in0=z_bank[g][:], scalar=-1.0, in1=nsp, op0=ALU.mult, op1=ALU.min)
 
-        def xy(h, g):
-            t = T[h]
-            nc.vector.scalar_tensor_tensor(out=t["xy"][:, g].rearrange("p k n -> p (k n)"), in0=t["q"][:, g].rearrange("p k n -> p (k n)"), scalar=1.0, in1=tb[g][:], op0=ALU.subtract, op1=ALU.mult)
+        def tangent(h, g):
+            t = work[h]
+            vec.scalar_tensor_tensor(
+                out=pair(t["nts"], g), in0=pair(t["q"], g), scalar=1.0, in1=tz_bank[g][:], op0=ALU.subtract, op1=ALU.mult
+            )
 
-        def gate(h, gs):
-            nc.scalar.activation(out=T[h]["s"][:, gs], in_=T[h]["d"][:, gs], func=ACT.Tanh, scale=0.5)
+        def z_difference(h, g):
+            t = work[h]
+            act.copy(out=t["z2"][:, g], in_=z_bank[g][:, W:])
+            vec.tensor_tensor(out=t["dz"][:, g], in0=z_bank[g][:, :W], in1=t["z2"][:, g], op=ALU.subtract)
 
-        def logq(h, g):
-            nc.scalar.activation(out=T[h]["p"][:, g], in_=T[h]["q"][:, g], func=ACT.Ln, bias=TINY)
+        def tz_difference(h, g):
+            t = work[h]
+            vec.tensor_tensor(out=t["dtz"][:, g], in0=tz_bank[g][:, :W], in1=t["tz2"][:, g], op=ALU.subtract)
 
-        def soft(h, g):
-            v = T[h]["p"][:, g].rearrange("p k n -> p (k n)")
-            nc.vector.scalar_tensor_tensor(out=v, in0=zb[g][:], scalar=-1.0, in1=v, op0=ALU.mult, op1=ALU.min)
+        def soft_product(h, gs):
+            t = work[h]
+            gps.tensor_tensor(out=t["sp"][:, gs], in0=t["nsp"][:, gs, 0], in1=t["nsp"][:, gs, 1], op=ALU.mult)
 
-        def tt(eng, o, a, b, op):
-            eng.tensor_tensor(out=o, in0=a, in1=b, op=op)
+        def cross_first(h, gs, engine):
+            t = work[h]
+            engine.tensor_tensor(out=t["acc"][:, gs], in0=t["nts"][:, gs, 0], in1=t["nsp"][:, gs, 1], op=ALU.mult)
 
-        def prod(h, gs, eng):
-            t = T[h]
-            tt(eng, t["m"][:, gs], t["p"][:, gs, 0], t["p"][:, gs, 1], ALU.mult)
+        def cross_second(h, gs):
+            t = work[h]
+            vec.tensor_tensor(out=t["cross"][:, gs], in0=t["nts"][:, gs, 1], in1=t["nsp"][:, gs, 0], op=ALU.mult)
 
-        def logs(h, g):
-            t = T[h]
-            nc.scalar.activation(out=t["L"][:, g], in_=t["m"][:, g], func=ACT.Ln, scale=gn_sb[:, g, 0:1], bias=1.0)
+        def cross_sum(h, gs):
+            t = work[h]
+            vec.tensor_tensor(out=t["acc"][:, gs], in0=t["acc"][:, gs], in1=t["cross"][:, gs], op=ALU.add)
 
-        def recip(h, gs):
-            t = T[h]
-            nc.scalar.activation(out=t["r"][:, gs], in_=t["L"][:, gs], func=ACT.Exp, scale=-1.0)
+        def logarithm(h, g):
+            t = work[h]
+            act.activation(out=t["lg"][:, g], in_=t["sp"][:, g], func=ACT.Ln, scale=gn_col[:, g, 0:1], bias=1.0)
 
-        def cu(h, gs, eng):
-            t = T[h]
-            tt(eng, t["u"][:, gs], t["xy"][:, gs, 0], t["p"][:, gs, 1], ALU.mult)
+        def gate_and_inverse(h, gs):
+            t = work[h]
+            act.activation(out=t["th"][:, gs], in_=t["dz"][:, gs], func=ACT.Tanh, scale=0.5)
+            act.activation(out=t["inv"][:, gs], in_=t["lg"][:, gs], func=ACT.Exp, scale=-1.0)
 
-        def cv(h, gs, eng):
-            t = T[h]
-            tt(eng, t["v"][:, gs], t["xy"][:, gs, 1], t["p"][:, gs, 0], ALU.mult)
+        def gate_slope(h, gs):
+            t = work[h]
+            vec.scalar_tensor_tensor(
+                out=t["sp"][:, gs], in0=t["th"][:, gs], scalar=1.0, in1=t["lg"][:, gs], op0=ALU.subtract, op1=ALU.mult
+            )
 
-        def csum(h, gs, eng):
-            t = T[h]
-            tt(eng, t["u"][:, gs], t["u"][:, gs], t["v"][:, gs], ALU.add)
+        def gate_term(h, g):
+            t = work[h]
+            vec.scalar_tensor_tensor(
+                out=t["dtz"][:, g], in0=t["dtz"][:, g], scalar=quarter_og[:, g, 0:1], in1=t["sp"][:, g], op0=ALU.mult, op1=ALU.mult
+            )
 
-        def bterm(h, gs):
-            t = T[h]
-            nc.vector.scalar_tensor_tensor(out=t["m"][:, gs], in0=t["s"][:, gs], scalar=1.0, in1=t["L"][:, gs], op0=ALU.subtract, op1=ALU.mult)
+        def log_term(h, g):
+            t = work[h]
+            vec.scalar_tensor_tensor(
+                out=t["acc"][:, g], in0=t["acc"][:, g], scalar=half_gn_og[:, g, 0:1], in1=t["inv"][:, g], op0=ALU.mult, op1=ALU.mult
+            )
 
-        def bterm2(h, g):
-            t = T[h]
-            nc.vector.scalar_tensor_tensor(out=t["dt"][:, g], in0=t["dt"][:, g], scalar=oq[:, g, 0:1], in1=t["m"][:, g], op0=ALU.mult, op1=ALU.mult)
+        def join_terms(h, gs):
+            t = work[h]
+            vec.tensor_tensor(out=t["acc"][:, gs], in0=t["acc"][:, gs], in1=t["dtz"][:, gs], op=ALU.subtract)
 
-        def wr(h, g):
-            t = T[h]
-            nc.vector.scalar_tensor_tensor(out=t["u"][:, g], in0=t["u"][:, g], scalar=cc[:, g, 0:1], in1=t["r"][:, g], op0=ALU.mult, op1=ALU.mult)
+        def apply_gate(h, gs):
+            t = work[h]
+            vec.scalar_tensor_tensor(
+                out=t["acc"][:, gs], in0=t["th"][:, gs], scalar=1.0, in1=t["acc"][:, gs], op0=ALU.add, op1=ALU.mult
+            )
 
-        def fin(k, h, gs, eng):
-            t = T[h]
-            other, op = [(t["dt"][:, gs], ALU.subtract), (None, None), (bs[:, gs, cols[h]], ALU.add)][k]
-            if k == 1:
-                eng.scalar_tensor_tensor(out=t["u"][:, gs], in0=t["s"][:, gs], scalar=1.0, in1=t["u"][:, gs], op0=ALU.add, op1=ALU.mult)
-            else:
-                tt(eng, t["u"][:, gs], t["u"][:, gs], other, op)
+        def add_base(h, gs, engine):
+            acc = work[h]["acc"][:, gs]
+            engine.tensor_tensor(out=acc, in0=acc, in1=base_sb[:, gs, cols[h]], op=ALU.add)
 
         def store(h, gs):
-            nc.sync.dma_start(out=out.rearrange("g m n -> m g n")[:, gs, cols[h]], in_=T[h]["u"][:, gs])
+            nc.sync.dma_start(out=out.rearrange("g m n -> m g n")[:, gs, cols[h]], in_=work[h]["acc"][:, gs])
 
+        low, high, every = slice(0, 2), slice(2, 4), slice(0, 4)
 
-        A, B, ALL = slice(0, 2), slice(2, 4), slice(0, 4)
-        V = nc.vector
-        PL = nc.gpsimd if POOL else V
-        V.transpose(out=gains[:], in_=gains_rows[:])
-        cast(dxs[0])
-        V.tensor_scalar(out=oq[:, :, 0:1], in0=og_sb[:, :, 0:1], scalar1=0.25, scalar2=None, op0=ALU.mult)
-        V.scalar_tensor_tensor(out=cc[:, :, 0:1], in0=gn_sb[:, :, 0:1], scalar=0.5, in1=og_sb[:, :, 0:1], op0=ALU.mult, op1=ALU.mult)
-        quant(dxs[0])
-        products(tb, (0, 1), dxs[0]); products(tb, (2, 3), dxs[0])
+        def log_table_phase(h, copied):
+            for g in range(G):
+                log_q(h, g)
+            for gs in (low, high):
+                for g in range(gs.start, gs.stop):
+                    softplus(h, g)
+                soft_product(h, gs)
+            cross_first(h, low, gps)
+            tangent(h, G - 1)
+            for g in range(G):
+                z_difference(h, g)
+            for g in range(copied, G):
+                act.copy(out=work[h]["tz2"][:, g], in_=tz_bank[g][:, W:])
+            for g in range(G):
+                tz_difference(h, g)
+            for g in range(G):
+                logarithm(h, g)
+
+        def cross_terms(h):
+            cross_second(h, every)
+            cross_first(h, high, vec)
+            cross_sum(h, low)
+            cross_sum(h, high)
+
+        vec.memset(gains_rows[:], 0.0)
+        for k, src in enumerate((gn, og)):
+            act.dma_start(
+                out=gains_rows[0:P:ROWS, k * M : k * M + M].rearrange("a (g i) -> a g i", g=G),
+                in_=src.rearrange("g (a i) o -> a g (i o)", i=ROWS),
+            )
+        load(x_first[0], x, slice(0, N_MM))
+        load(weights[0], w1, slice(0, M))
+        load(weights[1], w2, slice(0, M))
+        load(x_first[1], x, slice(N_MM, W))
+        load(dxs[0], dx, cols[0])
+        load(x_second, x, cols[1])
+        load(dxs[1], dx, cols[1])
+        nc.sync.dma_start(out=base_sb[:], in_=base.rearrange("g m n -> m g n"))
+
+        interleave(x_first[0])
+        interleave(weights[0])
+        quantise(x_first[0])
+        interleave(weights[1])
+        quantise(weights[0])
+        quantise(weights[1])
+        products(z_bank, (0, 1), x_first[0], 0, N_MM)
+        products(z_bank, (2, 3), x_first[0], 0, N_MM)
+        interleave(x_first[1])
+        vec.transpose(out=gains[:], in_=gains_rows[:])
+        quantise(x_first[1])
         for g in range(G):
-            qact(0, g)
-        cast(xs[1]); xy(0, 0); quant(xs[1]); xy(0, 1); cast(dxs[1]); xy(0, 2)
-
-        def log_phase(h):
-            for g in range(G):
-                logq(h, g)
-            soft(h, 0); soft(h, 1); prod(h, A, PL); soft(h, 2); soft(h, 3); prod(h, B, PL); cu(h, A, PL)
-            xy(h, 3)
-            for g in range(G):
-                cb(h, g); dd(h, g)
-                if g % 2 and h == 0:
-                    products(zb, (g - 1, g), xs[1])
-            for g in range(G):
-                ct(h, g); dt(h, g)
-            for g in range(G):
-                logs(h, g)
-
-        def mid(h):
-            cv(h, ALL, V); cu(h, B, V); csum(h, A, V); csum(h, B, V)
-            gate(h, A); recip(h, A); gate(h, B); recip(h, B)
-
-        log_phase(0)
-        quant(dxs[1])
-        products(tb, (0, 1, 2, 3), dxs[1])
-        mid(0)
-        bterm(0, A); wr(0, 0); wr(0, 1); bterm2(0, 0); bterm2(0, 1); bterm(0, B); fin(0, 0, A, V); wr(0, 2); wr(0, 3); bterm2(0, 2); bterm2(0, 3); fin(1, 0, A, V)
+            sigmoid_piece(g, 0)
+            products(z_bank, (g,), x_first[1], N_MM, N_MM)
+        interleave(dxs[0])
+        vec.tensor_scalar(out=quarter_og[:, :, 0:1], in0=og_col[:, :, 0:1], scalar1=0.25, scalar2=None, op0=ALU.mult)
+        vec.scalar_tensor_tensor(
+            out=half_gn_og[:, :, 0:1], in0=gn_col[:, :, 0:1], scalar=0.5, in1=og_col[:, :, 0:1], op0=ALU.mult, op1=ALU.mult
+        )
+        quantise(dxs[0])
+        products(tz_bank, (0, 1), dxs[0])
+        products(tz_bank, (2, 3), dxs[0])
         for g in range(G):
-            qact(1, g)
-        fin(2, 0, A, PL)
-        xy(1, 0); xy(1, 1); xy(1, 2)
-        fin(0, 0, B, V); fin(1, 0, B, V)
-        fin(2, 0, B, PL)
-        store(0, ALL)
-        log_phase(1)
-        mid(1)
-        bterm(1, A); wr(1, 0); wr(1, 1); bterm2(1, 0); bterm2(1, 1); bterm(1, B); fin(0, 1, A, V); wr(1, 2); wr(1, 3); fin(1, 1, A, V); bterm2(1, 2); bterm2(1, 3); fin(2, 1, A, V)
-        store(1, A)
-        for k in range(3):
-            fin(k, 1, slice(2, 3), V); fin(k, 1, slice(3, 4), V)
-        store(1, slice(2, 3)); store(1, slice(3, 4))
+            sigmoid_piece(g, N_MM)
+        interleave(x_second)
+        interleave_on_gpsimd(dxs[1])
+        for g in range(G - 1):
+            tangent(0, g)
+        for g in range(VECTOR_COPIES):
+            vec.tensor_copy(out=work[0]["tz2"][:, g], in_=tz_bank[g][:, W:])
+
+        log_table_phase(0, VECTOR_COPIES)
+        quantise(x_second)
+        quantise(dxs[1])
+        products(z_bank, range(G), x_second)
+        products(tz_bank, range(G), dxs[1])
+
+        cross_terms(0)
+        gate_and_inverse(0, every)
+        gate_slope(0, low)
+        log_term(0, 0)
+        log_term(0, 1)
+        gate_term(0, 0)
+        gate_term(0, 1)
+        gate_slope(0, high)
+        join_terms(0, low)
+        log_term(0, 2)
+        log_term(0, 3)
+        gate_term(0, 2)
+        gate_term(0, 3)
+        apply_gate(0, low)
+        join_terms(0, high)
+
+        for g in range(G):
+            sigmoid(1, g)
+        add_base(0, low, gps)
+        for g in range(G - 1):
+            tangent(1, g)
+        apply_gate(0, high)
+        add_base(0, high, gps)
+        store(0, every)
+
+        log_table_phase(1, 0)
+        cross_terms(1)
+        gate_and_inverse(1, low)
+        gate_and_inverse(1, high)
+        gate_slope(1, low)
+        log_term(1, 0)
+        log_term(1, 1)
+        gate_term(1, 0)
+        gate_term(1, 1)
+        gate_slope(1, high)
+        join_terms(1, low)
+        log_term(1, 2)
+        log_term(1, 3)
+        apply_gate(1, low)
+        gate_term(1, 2)
+        gate_term(1, 3)
+        add_base(1, low, vec)
+        store(1, low)
+        last = (slice(2, 3), slice(3, 4))
+        for gs in last:
+            join_terms(1, gs)
+        for gs in last:
+            apply_gate(1, gs)
+        for gs in last:
+            add_base(1, gs, vec)
+        for gs in last:
+            store(1, gs)

from contextlib import ExitStack

import concourse.mybir as mybir

F32 = mybir.dt.float32
BF16 = mybir.dt.bfloat16
U32 = mybir.dt.uint32
U8 = mybir.dt.uint8
FP8X4 = mybir.dt.float8_e4m3fn_x4
ALU = mybir.AluOpType
ACT = mybir.ActivationFunctionType

G, D, M, N = 4, 128, 128, 512
FLOPS = 4 * 2 * G * D * M * N

P = 128
ROWS = 32
PACK = 4
W = 256
N_MM = 128
TINY = 2.0**-40
VECTOR_COPIES = 2


def tile_rows_tnsoftprod_kernel(tc, x, w1, w2, gn, dx, og, base, out):
    nc = tc.nc
    vec, act, gps = nc.vector, nc.scalar, nc.gpsimd
    with ExitStack() as ctx:
        sb = ctx.enter_context(tc.tile_pool(name="sb", bufs=1))
        ps = ctx.enter_context(tc.psum_pool(name="ps", bufs=1))
        ctx.enter_context(tc.manual_schedule())

        def f32(name, *shape):
            return sb.tile([P, *shape], F32, name=name, align_bytes=64)

        def operand(name, width):
            return dict(
                raw=f32(name + "_raw", PACK, width),
                grouped=sb.tile([P, width, PACK], BF16, name=name + "_bf", align_bytes=64),
                codes=sb.tile([P, width], U32, name=name + "_codes", align_bytes=64),
                scales=sb.tile([P, width], U8, name=name + "_scales", align_bytes=64),
            )

        def load(opnd, src, cols):
            rows = src.rearrange("g (p j) n -> (g p) j n", j=PACK)
            nc.sync.dma_start(out=opnd["raw"][:], in_=rows[:, :, cols])

        def interleave(opnd):
            vec.tensor_copy(
                out=opnd["grouped"][:].rearrange("p (c i) j -> p c j i", i=4),
                in_=opnd["raw"][:].rearrange("p j (c i) -> p c j i", i=4),
            )

        def interleave_on_gpsimd(opnd):
            gps.tensor_scalar(
                out=opnd["grouped"][:],
                in0=opnd["raw"][:].rearrange("p j n -> p n j"),
                scalar1=1.0,
                scalar2=0.0,
                op0=ALU.mult,
                op1=ALU.add,
            )

        def quantise(opnd):
            vec.quantize_mx(
                out=opnd["codes"][:].bitcast(FP8X4),
                scales=opnd["scales"][:],
                in_=opnd["grouped"][:].rearrange("p n j -> p (n j)"),
            )

        def products(banks, groups, moving, first=0, width=W):
            for k, weight in enumerate(weights):
                for c in range(0, width, N_MM):
                    for g in groups:
                        rows = slice(ROWS * g, ROWS * g + ROWS)
                        at = k * W + first + c
                        nc.tensor.matmul_mx(
                            out=banks[g][:, at : at + N_MM],
                            lhsT=weight["codes"][rows, :].bitcast(FP8X4),
                            lhsT_scale=weight["scales"][rows, :],
                            rhs=moving["codes"][rows, c : c + N_MM].bitcast(FP8X4),
                            rhs_scale=moving["scales"][rows, c : c + N_MM],
                            start=True,
                            stop=True,
                        )

        weights = [operand("w1", M), operand("w2", M)]
        x_first = [operand("xa", N_MM), operand("xb", N_MM)]
        x_second = operand("x1", W)
        dxs = [operand("dx0", W), operand("dx1", W)]
        z_bank = [ps.tile([P, 2 * W], F32, name="z%d" % g) for g in range(G)]
        tz_bank = [ps.tile([P, 2 * W], F32, name="t%d" % g) for g in range(G)]
        cols = [slice(h * W, h * W + W) for h in range(2)]

        gains_rows = f32("gains_rows", 2 * M)
        gains = f32("gains", 2 * M)
        gn_col = gains[:, :M].rearrange("p (g i) -> p g i", g=G)
        og_col = gains[:, M:].rearrange("p (g i) -> p g i", g=G)
        half_gn_og = f32("cc", G, 8)
        quarter_og = f32("oq", G, 8)
        base_sb = f32("bs", G, N)

        work = []
        for h in range(2):
            tiles = {k: f32("%s%d" % (k, h), G, W) for k in ("z2", "tz2", "dz", "th", "dtz", "sp", "lg", "inv", "acc", "cross")}
            for k in ("q", "nsp", "nts"):
                tiles[k] = f32("%s%d" % (k, h), G, 2, W)
            work.append(tiles)

        def pair(tile, g):
            return tile[:, g].rearrange("p k n -> p (k n)")

        def sigmoid_piece(g, first):
            z = z_bank[g][:].rearrange("p (k n) -> p k n", k=2)
            piece = slice(first, first + N_MM)
            act.activation(out=work[0]["q"][:, g, :, piece], in_=z[:, :, piece], func=ACT.Sigmoid, scale=-1.0)

        def sigmoid(h, g):
            act.activation(out=pair(work[h]["q"], g), in_=z_bank[g][:], func=ACT.Sigmoid, scale=-1.0)

        def log_q(h, g):
            act.activation(out=work[h]["nsp"][:, g], in_=work[h]["q"][:, g], func=ACT.Ln, bias=TINY)

        def softplus(h, g):
            nsp = pair(work[h]["nsp"], g)
            vec.scalar_tensor_tensor(out=nsp, in0=z_bank[g][:], scalar=-1.0, in1=nsp, op0=ALU.mult, op1=ALU.min)

        def tangent(h, g):
            t = work[h]
            vec.scalar_tensor_tensor(
                out=pair(t["nts"], g), in0=pair(t["q"], g), scalar=1.0, in1=tz_bank[g][:], op0=ALU.subtract, op1=ALU.mult
            )

        def z_difference(h, g):
            t = work[h]
            act.copy(out=t["z2"][:, g], in_=z_bank[g][:, W:])
            vec.tensor_tensor(out=t["dz"][:, g], in0=z_bank[g][:, :W], in1=t["z2"][:, g], op=ALU.subtract)

        def tz_difference(h, g):
            t = work[h]
            vec.tensor_tensor(out=t["dtz"][:, g], in0=tz_bank[g][:, :W], in1=t["tz2"][:, g], op=ALU.subtract)

        def soft_product(h, gs):
            t = work[h]
            gps.tensor_tensor(out=t["sp"][:, gs], in0=t["nsp"][:, gs, 0], in1=t["nsp"][:, gs, 1], op=ALU.mult)

        def cross_first(h, gs, engine):
            t = work[h]
            engine.tensor_tensor(out=t["acc"][:, gs], in0=t["nts"][:, gs, 0], in1=t["nsp"][:, gs, 1], op=ALU.mult)

        def cross_second(h, gs):
            t = work[h]
            vec.tensor_tensor(out=t["cross"][:, gs], in0=t["nts"][:, gs, 1], in1=t["nsp"][:, gs, 0], op=ALU.mult)

        def cross_sum(h, gs):
            t = work[h]
            vec.tensor_tensor(out=t["acc"][:, gs], in0=t["acc"][:, gs], in1=t["cross"][:, gs], op=ALU.add)

        def logarithm(h, g):
            t = work[h]
            act.activation(out=t["lg"][:, g], in_=t["sp"][:, g], func=ACT.Ln, scale=gn_col[:, g, 0:1], bias=1.0)

        def gate_and_inverse(h, gs):
            t = work[h]
            act.activation(out=t["th"][:, gs], in_=t["dz"][:, gs], func=ACT.Tanh, scale=0.5)
            act.activation(out=t["inv"][:, gs], in_=t["lg"][:, gs], func=ACT.Exp, scale=-1.0)

        def gate_slope(h, gs):
            t = work[h]
            vec.scalar_tensor_tensor(
                out=t["sp"][:, gs], in0=t["th"][:, gs], scalar=1.0, in1=t["lg"][:, gs], op0=ALU.subtract, op1=ALU.mult
            )

        def gate_term(h, g):
            t = work[h]
            vec.scalar_tensor_tensor(
                out=t["dtz"][:, g], in0=t["dtz"][:, g], scalar=quarter_og[:, g, 0:1], in1=t["sp"][:, g], op0=ALU.mult, op1=ALU.mult
            )

        def log_term(h, g):
            t = work[h]
            vec.scalar_tensor_tensor(
                out=t["acc"][:, g], in0=t["acc"][:, g], scalar=half_gn_og[:, g, 0:1], in1=t["inv"][:, g], op0=ALU.mult, op1=ALU.mult
            )

        def join_terms(h, gs):
            t = work[h]
            vec.tensor_tensor(out=t["acc"][:, gs], in0=t["acc"][:, gs], in1=t["dtz"][:, gs], op=ALU.subtract)

        def apply_gate(h, gs):
            t = work[h]
            vec.scalar_tensor_tensor(
                out=t["acc"][:, gs], in0=t["th"][:, gs], scalar=1.0, in1=t["acc"][:, gs], op0=ALU.add, op1=ALU.mult
            )

        def add_base(h, gs, engine):
            acc = work[h]["acc"][:, gs]
            engine.tensor_tensor(out=acc, in0=acc, in1=base_sb[:, gs, cols[h]], op=ALU.add)

        def store(h, gs):
            nc.sync.dma_start(out=out.rearrange("g m n -> m g n")[:, gs, cols[h]], in_=work[h]["acc"][:, gs])

        low, high, every = slice(0, 2), slice(2, 4), slice(0, 4)

        def log_table_phase(h, copied):
            for g in range(G):
                log_q(h, g)
            for gs in (low, high):
                for g in range(gs.start, gs.stop):
                    softplus(h, g)
                soft_product(h, gs)
            cross_first(h, low, gps)
            tangent(h, G - 1)
            for g in range(G):
                z_difference(h, g)
            for g in range(copied, G):
                act.copy(out=work[h]["tz2"][:, g], in_=tz_bank[g][:, W:])
            for g in range(G):
                tz_difference(h, g)
            for g in range(G):
                logarithm(h, g)

        def cross_terms(h):
            cross_second(h, every)
            cross_first(h, high, vec)
            cross_sum(h, low)
            cross_sum(h, high)

        vec.memset(gains_rows[:], 0.0)
        for k, src in enumerate((gn, og)):
            act.dma_start(
                out=gains_rows[0:P:ROWS, k * M : k * M + M].rearrange("a (g i) -> a g i", g=G),
                in_=src.rearrange("g (a i) o -> a g (i o)", i=ROWS),
            )
        load(x_first[0], x, slice(0, N_MM))
        load(weights[0], w1, slice(0, M))
        load(weights[1], w2, slice(0, M))
        load(x_first[1], x, slice(N_MM, W))
        load(dxs[0], dx, cols[0])
        load(x_second, x, cols[1])
        load(dxs[1], dx, cols[1])
        nc.sync.dma_start(out=base_sb[:], in_=base.rearrange("g m n -> m g n"))

        interleave(x_first[0])
        interleave(weights[0])
        quantise(x_first[0])
        interleave(weights[1])
        quantise(weights[0])
        quantise(weights[1])
        products(z_bank, (0, 1), x_first[0], 0, N_MM)
        products(z_bank, (2, 3), x_first[0], 0, N_MM)
        interleave(x_first[1])
        vec.transpose(out=gains[:], in_=gains_rows[:])
        quantise(x_first[1])
        for g in range(G):
            sigmoid_piece(g, 0)
            products(z_bank, (g,), x_first[1], N_MM, N_MM)
        interleave(dxs[0])
        vec.tensor_scalar(out=quarter_og[:, :, 0:1], in0=og_col[:, :, 0:1], scalar1=0.25, scalar2=None, op0=ALU.mult)
        vec.scalar_tensor_tensor(
            out=half_gn_og[:, :, 0:1], in0=gn_col[:, :, 0:1], scalar=0.5, in1=og_col[:, :, 0:1], op0=ALU.mult, op1=ALU.mult
        )
        quantise(dxs[0])
        products(tz_bank, (0, 1), dxs[0])
        products(tz_bank, (2, 3), dxs[0])
        for g in range(G):
            sigmoid_piece(g, N_MM)
        interleave(x_second)
        interleave_on_gpsimd(dxs[1])
        for g in range(G - 1):
            tangent(0, g)
        for g in range(VECTOR_COPIES):
            vec.tensor_copy(out=work[0]["tz2"][:, g], in_=tz_bank[g][:, W:])

        log_table_phase(0, VECTOR_COPIES)
        quantise(x_second)
        quantise(dxs[1])
        products(z_bank, range(G), x_second)
        products(tz_bank, range(G), dxs[1])

        cross_terms(0)
        gate_and_inverse(0, every)
        gate_slope(0, low)
        log_term(0, 0)
        log_term(0, 1)
        gate_term(0, 0)
        gate_term(0, 1)
        gate_slope(0, high)
        join_terms(0, low)
        log_term(0, 2)
        log_term(0, 3)
        gate_term(0, 2)
        gate_term(0, 3)
        apply_gate(0, low)
        join_terms(0, high)

        for g in range(G):
            sigmoid(1, g)
        add_base(0, low, gps)
        for g in range(G - 1):
            tangent(1, g)
        apply_gate(0, high)
        add_base(0, high, gps)
        store(0, every)

        log_table_phase(1, 0)
        cross_terms(1)
        gate_and_inverse(1, low)
        gate_and_inverse(1, high)
        gate_slope(1, low)
        log_term(1, 0)
        log_term(1, 1)
        gate_term(1, 0)
        gate_term(1, 1)
        gate_slope(1, high)
        join_terms(1, low)
        log_term(1, 2)
        log_term(1, 3)
        apply_gate(1, low)
        gate_term(1, 2)
        gate_term(1, 3)
        add_base(1, low, vec)
        store(1, low)
        last = (slice(2, 3), slice(3, 4))
        for gs in last:
            join_terms(1, gs)
        for gs in last:
            apply_gate(1, gs)
        for gs in last:
            add_base(1, gs, vec)
        for gs in last:
            store(1, gs)
